import numpy as np
import ml_dtypes

BF16 = ml_dtypes.bfloat16


def bf(x):
    return np.asarray(x, np.float32).astype(BF16)


def f32(x):
    return np.asarray(x, np.float32)


def f64(x):
    return np.asarray(x).astype(np.float64)


def striped(idx):
    return np.tile(idx.reshape(-1, 16).T, (8, 1))


S, K, M, N, V, D = 256, 128, 256, 512, 64, 8


def gelu_tanh(v):
    return 0.5 * v * (1.0 + np.tanh(np.sqrt(2.0 / np.pi) * (v + 0.044715 * v**3)))


def setup_inputs():
    return {"table": bf(np.random.standard_normal((K, S))), "w": bf(np.random.standard_normal((K, M)) / np.sqrt(K)), "c": f32((0.2 + 0.8 * np.random.random_sample((1, N))) / np.sqrt(D)), "b": f32(0.5 * np.random.standard_normal((M, 1))), "offs": striped(np.random.permutation(np.tile(np.arange(S), 2))[:N])}


def reference(table, w, c, b, offs):
    idx = offs[:16].T.reshape(-1)
    y = (f64(w).T @ f64(table)[:, idx]).reshape(M, V, D)
    a = f64(c).reshape(V, D)
    z = (y * a).sum(axis=2)
    return gelu_tanh(z + f64(b))

@@ -1,0 +1,55 @@
+import concourse.mybir as mybir
+
+F32 = mybir.dt.float32
+BF16 = mybir.dt.bfloat16
+U16 = mybir.dt.uint16
+P = 128
+BAG = 8
+PER_COLUMN = 16
+
+FLOPS = 2 * 128 * 256 * 512 + 2 * 256 * 512
+
+
+def tile_rows_wbag_gelu_rep_kernel(tc, table, w, c, b, offs, out):
+    nc = tc.nc
+    words = table.shape[1]
+    blocks = w.shape[1] // P
+    entries = c.shape[1]
+    piece = words
+    pieces = entries // piece
+    bags = entries // BAG
+    piece_bags = piece // BAG
+    piece_columns = piece // PER_COLUMN
+
+    with (
+        tc.tile_pool(name="held", bufs=1) as held,
+        tc.psum_pool(name="psum", bufs=1) as psum,
+    ):
+        table_t = held.tile([P, words], BF16, name="table_t")
+        offsets = held.tile([P, entries // PER_COLUMN], U16, name="offsets")
+        w_t = held.tile([P, blocks * P], BF16, name="w_t")
+        c_t = held.tile([P, entries], F32, name="c_t")
+        b_t = held.tile([P, blocks], F32, name="b_t")
+
+        nc.sync.dma_start(table_t[:], table)
+        nc.scalar.dma_start(w_t[:], w)
+        nc.sync.dma_start(offsets[:], offs)
+        nc.sync.dma_start(c_t[:], c[0].partition_broadcast(P))
+        nc.scalar.dma_start(b_t[:], b.rearrange("(a p) o -> p (a o)", p=P))
+
+        for m in range(blocks):
+            z = held.tile([P, bags], F32, name=f"z{m}")
+            for s in range(pieces):
+                y = psum.tile([P, piece], F32, name=f"y{m}_{s}")
+                picked = table_t[:].indirect(offsets[:, s * piece_columns:(s + 1) * piece_columns])
+                nc.tensor.matmul(y[:], w_t[:, m * P:(m + 1) * P], picked, start=True, stop=True)
+                weighted = held.tile([P, piece], F32, name=f"weighted{m}_{s}")
+                nc.vector.tensor_tensor(weighted[:], y[:], c_t[:, s * piece:(s + 1) * piece],
+                                        mybir.AluOpType.mult)
+                nc.vector.tensor_reduce(z[:, s * piece_bags:(s + 1) * piece_bags],
+                                        weighted[:].rearrange("p (v t) -> p v t", t=BAG),
+                                        mybir.AxisListType.X, mybir.AluOpType.add)
+            result = held.tile([P, bags], F32, name=f"result{m}")
+            nc.scalar.activation(result[:], z[:], mybir.ActivationFunctionType.Gelu_apprx_tanh,
+                                 bias=b_t[:, m:m + 1])
+            nc.sync.dma_start(out[m * P:(m + 1) * P, :], result[:])

@@ -17,6 +17,8 @@ def tile_rows_wbag_gelu_rep_kernel(tc, table, w, c, b, offs, out):
     entries = c.shape[1]
     piece = words
     pieces = entries // piece
+    run = entries // P
+    piece_rows = piece // run
     bags = entries // BAG
     piece_bags = piece // BAG
     piece_columns = piece // PER_COLUMN
@@ -28,28 +30,50 @@ def tile_rows_wbag_gelu_rep_kernel(tc, table, w, c, b, offs, out):
         table_t = held.tile([P, words], BF16, name="table_t")
         offsets = held.tile([P, entries // PER_COLUMN], U16, name="offsets")
         w_t = held.tile([P, blocks * P], BF16, name="w_t")
-        c_t = held.tile([P, entries], F32, name="c_t")
+        c_down = held.tile([P, run], F32, name="c_down")
         b_t = held.tile([P, blocks], F32, name="b_t")
+        identity = held.tile([P, P], F32, name="identity")
 
-        nc.sync.dma_start(table_t[:], table)
+        nc.sync.dma_start(c_down[:], c.rearrange("o (p r) -> p (o r)", p=P))
         nc.scalar.dma_start(w_t[:], w)
+        nc.sync.dma_start(table_t[:], table)
         nc.sync.dma_start(offsets[:], offs)
-        nc.sync.dma_start(c_t[:], c[0].partition_broadcast(P))
         nc.scalar.dma_start(b_t[:], b.rearrange("(a p) o -> p (a o)", p=P))
 
-        for m in range(blocks):
-            z = held.tile([P, bags], F32, name=f"z{m}")
-            for s in range(pieces):
-                y = psum.tile([P, piece], F32, name=f"y{m}_{s}")
-                picked = table_t[:].indirect(offsets[:, s * piece_columns:(s + 1) * piece_columns])
+        ones = held.tile([P, P], F32, name="ones")
+        mean = held.tile([P, 2], BF16, name="mean")
+        column = held.tile([P, P], BF16, name="column")
+        partition = psum.tile([P, 2], F32, name="partition")
+        nc.vector.memset(ones[:], 1.0)
+        nc.vector.memset(mean[:], 1.0 / P)
+        nc.vector.tensor_tensor_scan(column[:], ones[:], ones[:], -1.0,
+                                     mybir.AluOpType.mult, mybir.AluOpType.add)
+        nc.tensor.matmul(partition[:], column[:], mean[:], start=True, stop=True)
+        nc.vector.tensor_single_scalar(identity[:], column[:], partition[:, 0:1],
+                                       mybir.AluOpType.is_equal)
+
+        c_rows = psum.tile([P, run, P], F32, name="c_rows")
+        for r in range(run):
+            nc.tensor.transpose(c_rows[:, r, :], c_down[:, r:r + 1].to_broadcast([P, P]), identity[:])
+
+        z = [held.tile([P, bags], F32, name=f"z{m}") for m in range(blocks)]
+        for s in range(pieces):
+            c_t = held.tile([P, piece_rows, run], F32, name=f"c_t{s}")
+            nc.scalar.copy(c_t[:], c_rows[:, :, s * piece_rows:(s + 1) * piece_rows].rearrange("p r i -> p i r"))
+
+            picked = table_t[:].indirect(offsets[:, s * piece_columns:(s + 1) * piece_columns])
+            for m in range(blocks):
+                y = psum.tile([P, piece], F32, name=f"y{s}_{m}")
                 nc.tensor.matmul(y[:], w_t[:, m * P:(m + 1) * P], picked, start=True, stop=True)
-                weighted = held.tile([P, piece], F32, name=f"weighted{m}_{s}")
-                nc.vector.tensor_tensor(weighted[:], y[:], c_t[:, s * piece:(s + 1) * piece],
+                weighted = held.tile([P, piece], F32, name=f"weighted{s}_{m}")
+                nc.vector.tensor_tensor(weighted[:], y[:], c_t[:].rearrange("p i r -> p (i r)"),
                                         mybir.AluOpType.mult)
-                nc.vector.tensor_reduce(z[:, s * piece_bags:(s + 1) * piece_bags],
+                nc.vector.tensor_reduce(z[m][:, s * piece_bags:(s + 1) * piece_bags],
                                         weighted[:].rearrange("p (v t) -> p v t", t=BAG),
                                         mybir.AxisListType.X, mybir.AluOpType.add)
+
+        for m in range(blocks):
             result = held.tile([P, bags], F32, name=f"result{m}")
-            nc.scalar.activation(result[:], z[:], mybir.ActivationFunctionType.Gelu_apprx_tanh,
+            nc.scalar.activation(result[:], z[m][:], mybir.ActivationFunctionType.Gelu_apprx_tanh,
                                  bias=b_t[:, m:m + 1])
             nc.sync.dma_start(out[m * P:(m + 1) * P, :], result[:])

@@ -68,8 +68,13 @@ def tile_rows_wbag_gelu_rep_kernel(tc, table, w, c, b, offs, out):
                 weighted = held.tile([P, piece], F32, name=f"weighted{s}_{m}")
                 nc.vector.tensor_tensor(weighted[:], y[:], c_t[:].rearrange("p i r -> p (i r)"),
                                         mybir.AluOpType.mult)
-                nc.vector.tensor_reduce(z[m][:, s * piece_bags:(s + 1) * piece_bags],
-                                        weighted[:].rearrange("p (v t) -> p v t", t=BAG),
+                terms = weighted[:].rearrange("p (v t) -> p v t", t=BAG)
+                if s < pieces - 1:
+                    halves = held.tile([P, piece_bags, BAG // 2], F32, name=f"halves{s}_{m}")
+                    nc.gpsimd.tensor_tensor(halves[:], terms[:, :, :BAG // 2], terms[:, :, BAG // 2:],
+                                            mybir.AluOpType.add)
+                    terms = halves[:]
+                nc.vector.tensor_reduce(z[m][:, s * piece_bags:(s + 1) * piece_bags], terms,
                                         mybir.AxisListType.X, mybir.AluOpType.add)
 
         for m in range(blocks):

import concourse.mybir as mybir

F32 = mybir.dt.float32
BF16 = mybir.dt.bfloat16
U16 = mybir.dt.uint16
P = 128
BAG = 8
PER_COLUMN = 16

FLOPS = 2 * 128 * 256 * 512 + 2 * 256 * 512


def tile_rows_wbag_gelu_rep_kernel(tc, table, w, c, b, offs, out):
    nc = tc.nc
    words = table.shape[1]
    blocks = w.shape[1] // P
    entries = c.shape[1]
    piece = words
    pieces = entries // piece
    run = entries // P
    piece_rows = piece // run
    bags = entries // BAG
    piece_bags = piece // BAG
    piece_columns = piece // PER_COLUMN

    with (
        tc.tile_pool(name="held", bufs=1) as held,
        tc.psum_pool(name="psum", bufs=1) as psum,
    ):
        table_t = held.tile([P, words], BF16, name="table_t")
        offsets = held.tile([P, entries // PER_COLUMN], U16, name="offsets")
        w_t = held.tile([P, blocks * P], BF16, name="w_t")
        c_down = held.tile([P, run], F32, name="c_down")
        b_t = held.tile([P, blocks], F32, name="b_t")
        identity = held.tile([P, P], F32, name="identity")

        nc.sync.dma_start(c_down[:], c.rearrange("o (p r) -> p (o r)", p=P))
        nc.scalar.dma_start(w_t[:], w)
        nc.sync.dma_start(table_t[:], table)
        nc.sync.dma_start(offsets[:], offs)
        nc.scalar.dma_start(b_t[:], b.rearrange("(a p) o -> p (a o)", p=P))

        ones = held.tile([P, P], F32, name="ones")
        mean = held.tile([P, 2], BF16, name="mean")
        column = held.tile([P, P], BF16, name="column")
        partition = psum.tile([P, 2], F32, name="partition")
        nc.vector.memset(ones[:], 1.0)
        nc.vector.memset(mean[:], 1.0 / P)
        nc.vector.tensor_tensor_scan(column[:], ones[:], ones[:], -1.0,
                                     mybir.AluOpType.mult, mybir.AluOpType.add)
        nc.tensor.matmul(partition[:], column[:], mean[:], start=True, stop=True)
        nc.vector.tensor_single_scalar(identity[:], column[:], partition[:, 0:1],
                                       mybir.AluOpType.is_equal)

        c_rows = psum.tile([P, run, P], F32, name="c_rows")
        for r in range(run):
            nc.tensor.transpose(c_rows[:, r, :], c_down[:, r:r + 1].to_broadcast([P, P]), identity[:])

        z = [held.tile([P, bags], F32, name=f"z{m}") for m in range(blocks)]
        for s in range(pieces):
            c_t = held.tile([P, piece_rows, run], F32, name=f"c_t{s}")
            nc.scalar.copy(c_t[:], c_rows[:, :, s * piece_rows:(s + 1) * piece_rows].rearrange("p r i -> p i r"))

            picked = table_t[:].indirect(offsets[:, s * piece_columns:(s + 1) * piece_columns])
            for m in range(blocks):
                y = psum.tile([P, piece], F32, name=f"y{s}_{m}")
                nc.tensor.matmul(y[:], w_t[:, m * P:(m + 1) * P], picked, start=True, stop=True)
                weighted = held.tile([P, piece], F32, name=f"weighted{s}_{m}")
                nc.vector.tensor_tensor(weighted[:], y[:], c_t[:].rearrange("p i r -> p (i r)"),
                                        mybir.AluOpType.mult)
                terms = weighted[:].rearrange("p (v t) -> p v t", t=BAG)
                if s < pieces - 1:
                    halves = held.tile([P, piece_bags, BAG // 2], F32, name=f"halves{s}_{m}")
                    nc.gpsimd.tensor_tensor(halves[:], terms[:, :, :BAG // 2], terms[:, :, BAG // 2:],
                                            mybir.AluOpType.add)
                    terms = halves[:]
                nc.vector.tensor_reduce(z[m][:, s * piece_bags:(s + 1) * piece_bags], terms,
                                        mybir.AxisListType.X, mybir.AluOpType.add)

        for m in range(blocks):
            result = held.tile([P, bags], F32, name=f"result{m}")
            nc.scalar.activation(result[:], z[m][:], mybir.ActivationFunctionType.Gelu_apprx_tanh,
                                 bias=b_t[:, m:m + 1])
            nc.sync.dma_start(out[m * P:(m + 1) * P, :], result[:])
